import numpy as np
import ml_dtypes


def mxq(x, axis, fmt="e4m3"):
    dtype, down = {"e4m3": (ml_dtypes.float8_e4m3fn, 7), "e5m2": (ml_dtypes.float8_e5m2, 14)}[fmt]
    v = np.moveaxis(np.asarray(x, np.float32).astype(ml_dtypes.bfloat16).astype(np.float64), axis, -1)
    blocks = v.reshape(v.shape[:-1] + (-1, 32))
    amax = np.abs(blocks).max(-1, keepdims=True)
    byte = np.maximum(np.where(amax > 0, np.frexp(amax)[1] - 1 + 127, 0) - down, 1)
    scale = np.exp2(byte - 127.0)
    codes = (blocks / scale).astype(np.float32).astype(dtype).astype(np.float64)
    return np.moveaxis((codes * scale).reshape(v.shape), -1, axis)


WIDE = False


def mx_kscale(k):
    if not WIDE:
        return np.ones(k)
    levels = np.array([10, -10, 5, -5, 0])
    if k % 512:
        return np.exp2(np.random.permutation(np.resize(levels, k // 32))).repeat(32)
    a = np.empty((k // 512, 16))
    for p in range(k // 512):
        a[p, :8] = np.random.permutation(np.resize(levels, 8))
        for g in range(8):
            far = levels[np.abs(levels - a[p, g]) >= 10]
            a[p, g + 8] = far[np.random.randint(len(far))]
    return np.exp2(a.ravel()).repeat(32)


def f64(x):
    return np.asarray(x).astype(np.float64)


def striped8(idx):
    return np.asarray(idx).reshape(8, -1, 16).transpose(0, 2, 1).reshape(128, -1).astype(np.uint16)


def unstriped8(offs):
    return offs.reshape(8, 16, -1).transpose(0, 2, 1).reshape(8, -1).astype(np.int64)


def pick8(x, idx, run):
    r = np.arange(len(x))
    return x[r[:, None], idx[r % (8 * run) // run]]


E2M1 = np.array([0.0, 0.5, 1.0, 1.5, 2.0, 3.0, 4.0, 6.0, -0.0, -0.5, -1.0, -1.5, -2.0, -3.0, -4.0, -6.0])


def pack_weight(w, fmt):
    k, n = w.shape
    w = f64(np.asarray(w, np.float32).astype(ml_dtypes.bfloat16)).reshape(k // 32, 32, n)
    amax = np.abs(w).max(1)
    if fmt == "e4m3":
        byte = np.frexp(amax)[1] - 1 + 127 - 7
    else:
        mant, ex = np.frexp(amax / 6.0)
        byte = np.where(mant > 0.5, ex, ex - 1) + 127
    byte = np.clip(np.where(amax > 0, byte, 1), 1, 254)
    scaled = (w * np.exp2(127.0 - byte)[:, None, :]).reshape(k, n).astype(np.float32)
    by_word = np.ascontiguousarray(scaled.reshape(k // 512, 128, 4, n).transpose(0, 1, 3, 2))
    if fmt == "e4m3":
        words = by_word.astype(ml_dtypes.float8_e4m3fn).view(np.uint8)
    else:
        c = by_word.astype(ml_dtypes.float4_e2m1fn).view(np.uint8) & 0xF
        words = (c[..., 0::2] | (c[..., 1::2] << 4)).reshape(k // 512, 128, 2 * n)
    return np.ascontiguousarray(words), np.ascontiguousarray(byte.astype(np.uint8).reshape(k // 512, 16, n))


def unpack_weight(words, scales, fmt):
    g, _, n = scales.shape
    words = np.ascontiguousarray(words).reshape(g, 128, n, -1)
    if fmt == "e4m3":
        vals = words.view(ml_dtypes.float8_e4m3fn).astype(np.float64)
    else:
        nib = np.empty((g, 128, n, 4), np.uint8)
        nib[..., 0::2] = words & 0xF
        nib[..., 1::2] = words >> 4
        vals = E2M1[nib]
    vals = vals * np.repeat(np.exp2(scales.astype(np.float64) - 127.0), 8, axis=1)[..., None]
    return vals.transpose(0, 1, 3, 2).reshape(g * 512, n)


def softplus(v):
    return np.log(1.0 + np.exp(v))


D, T, I, Q = 512, 1024, 512, 128


def setup_inputs():
    n = np.random.standard_normal
    idx = np.stack([np.random.permutation(T)[:I] for _ in range(8)])
    idx2 = np.stack([np.random.permutation(T)[:I] for _ in range(8)])
    fd = mx_kscale(D)
    keysp = pack_weight(n((D, T)) / fd[:, None], "e4m3")
    return {
        "query": (n((D, Q)) * 0.9 / np.sqrt(D) * fd[:, None]).astype(np.float32),
        "query2": (n((D, Q)) * 0.9 / np.sqrt(D) * fd[:, None]).astype(np.float32),
        "keys_words": keysp[0],
        "keys_scales": keysp[1],
        "lam": (np.random.uniform(1.0, 2.0, (Q, 1))).astype(np.float32),
        "old": (1.0 * n((Q, T))).astype(np.float32),
        "share2": (np.random.uniform(0.4, 1.2, (Q, 1))).astype(np.float32),
        "offs": striped8(idx),
        "offs2": striped8(idx2),
    }


def reference(query, query2, keys_words, keys_scales, lam, old, share2, offs, offs2):
    idx = unstriped8(offs)
    idx2 = unstriped8(offs2)
    keysu = unpack_weight(keys_words, keys_scales, "e4m3")
    queryq = mxq(f64(query), 0, "e4m3")
    a = queryq.T @ keysu
    query2q = mxq(f64(query2), 0, "e4m3")
    b = query2q.T @ keysu
    ra = np.sqrt(softplus(pick8(a, idx, 16)) * softplus(pick8(b, idx, 16)) + 0.1)
    w = ra * f64(lam) - np.abs(pick8(a, idx, 16) - pick8(b, idx, 16))
    f1 = np.zeros((Q, T))
    f1[np.arange(Q)[:, None], idx[np.arange(Q) % 128 // 16]] = w
    f2 = np.zeros((Q, T))
    f2[np.arange(Q)[:, None], idx2[np.arange(Q) % 128 // 16]] = w
    y = f64(old) + f1 + f2 * f64(share2)
    return y

@@ -1,0 +1,141 @@
+from contextlib import ExitStack
+
+import concourse.mybir as mybir
+from concourse.masks import make_identity
+
+D, T, SLOTS, Q = 512, 1024, 512, 128
+FLOPS = 2 * 2 * D * Q * T
+
+F32 = mybir.dt.float32
+BF16 = mybir.dt.bfloat16
+I32 = mybir.dt.int32
+U16 = mybir.dt.uint16
+U8 = mybir.dt.uint8
+FP8X4 = mybir.dt.float8_e4m3fn_x4
+ACT = mybir.ActivationFunctionType
+ALU = mybir.AluOpType
+
+P = 128
+PACK = 4
+BANK = 512
+CHUNK = 256
+STORE = 256
+TINY = 1e-19
+
+
+def tile_attend_agreeingtwo_lean_twiceput_heads_kernel(tc, query, query2, keys_words, keys_scales, lam, old, share2, offs, offs2, out):
+    nc = tc.nc
+    with ExitStack() as ctx:
+        pool = ctx.enter_context(tc.tile_pool(name="pool", bufs=1))
+        psum = ctx.enter_context(tc.psum_pool(name="psum", bufs=1))
+
+        offs_sb = pool.tile([P, SLOTS // 16], U16, name="offs_sb")
+        offs2_sb = pool.tile([P, SLOTS // 16], U16, name="offs2_sb")
+        key_scale = pool.tile([P, T], U8, name="key_scale", align_bytes=64)
+        nc.gpsimd.memset(key_scale[:].bitcast(I32), 0)
+
+        nc.sync.dma_start(offs_sb[:], offs)
+        raw = [pool.tile([P, PACK, Q], F32, name="raw%d" % i) for i in range(2)]
+        for tile, src in zip(raw, (query, query2)):
+            nc.sync.dma_start(out=tile[:], in_=src.rearrange("(p j) q -> p j q", j=PACK))
+        scale_rows = keys_scales[0].bitcast(I32)
+        for quad in range(4):
+            nc.sync.dma_start(out=key_scale[32 * quad : 32 * quad + 4, :].bitcast(I32), in_=scale_rows[4 * quad : 4 * quad + 4, :])
+        words = keys_words[0].rearrange("p n t -> p (n t)").bitcast(I32)
+        key_code = [pool.tile([P, BANK], I32, name="key_code%d" % h, align_bytes=64) for h in range(T // BANK)]
+        for h, tile in enumerate(key_code):
+            nc.sync.dma_start(out=tile[:], in_=words[:, h * BANK : (h + 1) * BANK])
+        nc.sync.dma_start(offs2_sb[:], offs2)
+        lam_sb = pool.tile([P, 1], F32, name="lam_sb")
+        share_sb = pool.tile([P, 1], F32, name="share_sb")
+        old_sb = pool.tile([P, T], F32, name="old_sb")
+        nc.sync.dma_start(out=lam_sb[:], in_=lam)
+        nc.sync.dma_start(out=share_sb[:], in_=share2)
+        nc.sync.dma_start(out=old_sb[:], in_=old)
+
+        f1 = [pool.tile([P, T], F32, name="f1_%d" % n) for n in range(SLOTS // CHUNK)]
+        f2 = pool.tile([P, T], F32, name="f2")
+        for part in f1:
+            nc.vector.memset(part[:], 0.0)
+        nc.vector.memset(f2[:], 0.0)
+
+        q_code, q_scale = [], []
+        for i in range(2):
+            grouped = pool.tile([P, Q, PACK], BF16, name="grouped%d" % i, align_bytes=64)
+            nc.vector.tensor_copy(out=grouped[:].rearrange("p (c i) j -> p c j i", i=4), in_=raw[i][:].rearrange("p j (c i) -> p c j i", i=4))
+            code = pool.tile([P, Q], I32, name="q_code%d" % i, align_bytes=64)
+            scale = pool.tile([P, Q], U8, name="q_scale%d" % i, align_bytes=64)
+            nc.vector.quantize_mx(out=code[:].bitcast(FP8X4), scales=scale[:], in_=grouped[:].rearrange("p q j -> p (q j)"))
+            q_code.append(code)
+            q_scale.append(scale)
+
+        scores = [pool.tile([P, T], F32, name="scores%d" % i) for i in range(2)]
+        for i in range(2):
+            for h in range(T // BANK):
+                cols = slice(h * BANK, (h + 1) * BANK)
+                bank = psum.tile([P, BANK], F32, name="bank%d%d" % (i, h))
+                nc.tensor.matmul_mx(out=bank[:], lhsT=q_code[i][:].bitcast(FP8X4), lhsT_scale=q_scale[i][:],
+                                    rhs=key_code[h][:].bitcast(FP8X4), rhs_scale=key_scale[:, cols], start=True, stop=True)
+                nc.vector.tensor_copy(out=scores[i][:, cols], in_=bank[:])
+
+        sig = pool.tile([P, 2, SLOTS], F32, name="sig")
+        picked = pool.tile([P, 2, SLOTS], F32, name="picked")
+        for i in range(2):
+            nc.scalar.activation(sig[:, i, :], scores[i][:].indirect(offs_sb[:]), ACT.Sigmoid, scale=-1.0)
+        for i in range(2):
+            nc.vector.tensor_copy(picked[:, i, :], scores[i][:].indirect(offs_sb[:]))
+
+        chunks = [slice(c, c + CHUNK) for c in range(0, SLOTS, CHUNK)]
+        prods = []
+        for n, c in enumerate(chunks):
+            logsig = pool.tile([P, 2, CHUNK], F32, name="logsig%d" % n)
+            nc.scalar.activation(logsig[:], sig[:, :, c], ACT.Ln, bias=TINY)
+            soft = pool.tile([P, 2, CHUNK], F32, name="soft%d" % n)
+            nc.vector.scalar_tensor_tensor(soft[:], logsig[:], -1.0, picked[:, :, c], ALU.mult, ALU.max)
+            prod = pool.tile([P, CHUNK], F32, name="prod%d" % n)
+            nc.vector.tensor_tensor(prod[:], soft[:, 0, :], soft[:, 1, :], ALU.mult)
+            prods.append(prod)
+
+        diff = pool.tile([P, SLOTS], F32, name="diff")
+        nc.vector.tensor_tensor(diff[:], picked[:, 0, :], picked[:, 1, :], ALU.subtract)
+        minus_gap = pool.tile([P, SLOTS], F32, name="minus_gap")
+        nc.vector.scalar_tensor_tensor(minus_gap[:], diff[:], -1.0, diff[:], ALU.mult, ALU.min)
+
+        identity = pool.tile([P, P], F32, name="identity")
+        make_identity(nc, identity[:])
+        halves = range(T // BANK)
+        blocks = range(BANK // P)
+        turned = [psum.tile([P, BANK], F32, name="turned%d" % h) for h in halves]
+        for h in halves:
+            for j in blocks:
+                t0 = h * BANK + j * P
+                nc.tensor.matmul(turned[h][:, j * P : (j + 1) * P], old_sb[:, t0 : t0 + P], identity[:], start=(j == 0), stop=False, is_transpose=True)
+
+        scaled = pool.tile([P, SLOTS], F32, name="scaled")
+        for n, c in enumerate(chunks):
+            root = pool.tile([P, CHUNK], F32, name="root%d" % n)
+            nc.scalar.activation(root[:], prods[n][:], ACT.Sqrt, bias=0.1)
+            nc.scalar.activation(scaled[:, c], root[:], ACT.Copy, scale=lam_sb[:])
+            nc.vector.tensor_tensor(f1[n][:].indirect(offs_sb[:, c.start // 16 : c.stop // 16]), scaled[:, c], minus_gap[:, c], ALU.add)
+        nc.vector.tensor_tensor(f2[:].indirect(offs2_sb[:]), scaled[:], minus_gap[:], ALU.add)
+
+        for n, part in enumerate(f1):
+            for h in halves:
+                for j in blocks:
+                    t0 = h * BANK + j * P
+                    last = n == len(f1) - 1 and j == len(blocks) - 1
+                    nc.tensor.matmul(turned[h][:, j * P : (j + 1) * P], part[:, t0 : t0 + P], identity[:], start=False, stop=last, is_transpose=True)
+        partial = []
+        for h in halves:
+            turned_sb = pool.tile([P, BANK], F32, name="turned_sb%d" % h)
+            nc.scalar.copy(turned_sb[:], turned[h][:])
+            back = psum.tile([P, BANK], F32, name="back%d" % h)
+            for j in blocks:
+                nc.tensor.transpose(back[:, j * P : (j + 1) * P], turned_sb[:, j * P : (j + 1) * P], identity[:])
+            partial.append(back)
+        for n, c0 in enumerate(range(0, T, STORE)):
+            cols = slice(c0, c0 + STORE)
+            res = pool.tile([P, STORE], F32, name="res%d" % n)
+            nc.vector.scalar_tensor_tensor(res[:], f2[:, cols], share_sb[:], partial[c0 // BANK][:, c0 % BANK : c0 % BANK + STORE], ALU.mult, ALU.add)
+            queue = nc.sync if n % 2 == 0 else nc.scalar
+            queue.dma_start(out=out[:, cols], in_=res[:])

@@ -20,6 +20,7 @@ PACK = 4
 BANK = 512
 CHUNK = 256
 STORE = 256
+FIRST = 128
 TINY = 1e-19
 
 
@@ -34,15 +35,15 @@ def tile_attend_agreeingtwo_lean_twiceput_heads_kernel(tc, query, query2, keys_w
         key_scale = pool.tile([P, T], U8, name="key_scale", align_bytes=64)
         nc.gpsimd.memset(key_scale[:].bitcast(I32), 0)
 
-        nc.sync.dma_start(offs_sb[:], offs)
         raw = [pool.tile([P, PACK, Q], F32, name="raw%d" % i) for i in range(2)]
-        for tile, src in zip(raw, (query, query2)):
-            nc.sync.dma_start(out=tile[:], in_=src.rearrange("(p j) q -> p j q", j=PACK))
+        nc.sync.dma_start(out=raw[0][:], in_=query.rearrange("(p j) q -> p j q", j=PACK))
+        nc.sync.dma_start(offs_sb[:], offs)
+        nc.sync.dma_start(out=raw[1][:], in_=query2.rearrange("(p j) q -> p j q", j=PACK))
         scale_rows = keys_scales[0].bitcast(I32)
         for quad in range(4):
             nc.sync.dma_start(out=key_scale[32 * quad : 32 * quad + 4, :].bitcast(I32), in_=scale_rows[4 * quad : 4 * quad + 4, :])
         words = keys_words[0].rearrange("p n t -> p (n t)").bitcast(I32)
-        key_code = [pool.tile([P, BANK], I32, name="key_code%d" % h, align_bytes=64) for h in range(T // BANK)]
+        key_code = [pool.tile([P, BANK], I32, name="key_code%d" % h, tag="key_code%d" % h, align_bytes=64) for h in range(T // BANK)]
         for h, tile in enumerate(key_code):
             nc.sync.dma_start(out=tile[:], in_=words[:, h * BANK : (h + 1) * BANK])
         nc.sync.dma_start(offs2_sb[:], offs2)
@@ -54,14 +55,12 @@ def tile_attend_agreeingtwo_lean_twiceput_heads_kernel(tc, query, query2, keys_w
         nc.sync.dma_start(out=old_sb[:], in_=old)
 
         f1 = [pool.tile([P, T], F32, name="f1_%d" % n) for n in range(SLOTS // CHUNK)]
-        f2 = pool.tile([P, T], F32, name="f2")
         for part in f1:
             nc.vector.memset(part[:], 0.0)
-        nc.vector.memset(f2[:], 0.0)
 
         q_code, q_scale = [], []
         for i in range(2):
-            grouped = pool.tile([P, Q, PACK], BF16, name="grouped%d" % i, align_bytes=64)
+            grouped = pool.tile([P, Q, PACK], BF16, name="grouped%d" % i, tag="grouped%d" % i, align_bytes=64)
             nc.vector.tensor_copy(out=grouped[:].rearrange("p (c i) j -> p c j i", i=4), in_=raw[i][:].rearrange("p j (c i) -> p c j i", i=4))
             code = pool.tile([P, Q], I32, name="q_code%d" % i, align_bytes=64)
             scale = pool.tile([P, Q], U8, name="q_scale%d" % i, align_bytes=64)
@@ -69,32 +68,42 @@ def tile_attend_agreeingtwo_lean_twiceput_heads_kernel(tc, query, query2, keys_w
             q_code.append(code)
             q_scale.append(scale)
 
+        f2 = pool.tile([P, T], F32, name="f2", tag="grouped1", align_bytes=64)
+        nc.gpsimd.memset(f2[:], 0.0)
+
         scores = [pool.tile([P, T], F32, name="scores%d" % i) for i in range(2)]
+        pieces = ((256, 256, 512), (512, 256, 256))
+        banks = 0
         for i in range(2):
-            for h in range(T // BANK):
-                cols = slice(h * BANK, (h + 1) * BANK)
-                bank = psum.tile([P, BANK], F32, name="bank%d%d" % (i, h))
+            t0 = 0
+            for width in pieces[i]:
+                cols = slice(t0, t0 + width)
+                bank = psum.tile([P, width], F32, name="bank%d" % banks, tag="bank%d" % banks)
                 nc.tensor.matmul_mx(out=bank[:], lhsT=q_code[i][:].bitcast(FP8X4), lhsT_scale=q_scale[i][:],
-                                    rhs=key_code[h][:].bitcast(FP8X4), rhs_scale=key_scale[:, cols], start=True, stop=True)
+                                    rhs=key_code[t0 // BANK][:, t0 % BANK : t0 % BANK + width].bitcast(FP8X4), rhs_scale=key_scale[:, cols], start=True, stop=True)
                 nc.vector.tensor_copy(out=scores[i][:, cols], in_=bank[:])
+                t0 += width
+                banks += 1
 
         sig = pool.tile([P, 2, SLOTS], F32, name="sig")
-        picked = pool.tile([P, 2, SLOTS], F32, name="picked")
+        picked = pool.tile([P, 2, SLOTS], F32, name="picked", tag="key_code1", align_bytes=64)
+        halves_of_slots = [slice(c, c + CHUNK) for c in range(0, SLOTS, CHUNK)]
+
+        def entries(tile, slots):
+            return tile[:, slots.start // 16 : slots.stop // 16]
+
         for i in range(2):
             nc.scalar.activation(sig[:, i, :], scores[i][:].indirect(offs_sb[:]), ACT.Sigmoid, scale=-1.0)
         for i in range(2):
             nc.vector.tensor_copy(picked[:, i, :], scores[i][:].indirect(offs_sb[:]))
 
-        chunks = [slice(c, c + CHUNK) for c in range(0, SLOTS, CHUNK)]
-        prods = []
-        for n, c in enumerate(chunks):
+        prod = pool.tile([P, SLOTS], F32, name="prod")
+        for n, c in enumerate(halves_of_slots):
             logsig = pool.tile([P, 2, CHUNK], F32, name="logsig%d" % n)
             nc.scalar.activation(logsig[:], sig[:, :, c], ACT.Ln, bias=TINY)
             soft = pool.tile([P, 2, CHUNK], F32, name="soft%d" % n)
             nc.vector.scalar_tensor_tensor(soft[:], logsig[:], -1.0, picked[:, :, c], ALU.mult, ALU.max)
-            prod = pool.tile([P, CHUNK], F32, name="prod%d" % n)
-            nc.vector.tensor_tensor(prod[:], soft[:, 0, :], soft[:, 1, :], ALU.mult)
-            prods.append(prod)
+            nc.vector.tensor_tensor(prod[:, c], soft[:, 0, :], soft[:, 1, :], ALU.mult)
 
         diff = pool.tile([P, SLOTS], F32, name="diff")
         nc.vector.tensor_tensor(diff[:], picked[:, 0, :], picked[:, 1, :], ALU.subtract)
@@ -103,39 +112,43 @@ def tile_attend_agreeingtwo_lean_twiceput_heads_kernel(tc, query, query2, keys_w
 
         identity = pool.tile([P, P], F32, name="identity")
         make_identity(nc, identity[:])
-        halves = range(T // BANK)
-        blocks = range(BANK // P)
-        turned = [psum.tile([P, BANK], F32, name="turned%d" % h) for h in halves]
-        for h in halves:
-            for j in blocks:
-                t0 = h * BANK + j * P
-                nc.tensor.matmul(turned[h][:, j * P : (j + 1) * P], old_sb[:, t0 : t0 + P], identity[:], start=(j == 0), stop=False, is_transpose=True)
+        pieces_out = range(T // STORE)
+        blocks = range(STORE // P)
+        turned = [psum.tile([P, STORE], F32, name="turned%d" % h, tag="bank%d" % h) for h in pieces_out]
 
+        def add_turned(source, opens, closes):
+            for h in pieces_out:
+                for j in blocks:
+                    t0 = h * STORE + j * P
+                    nc.tensor.matmul(turned[h][:, j * P : (j + 1) * P], source[:, t0 : t0 + P], identity[:],
+                                     start=opens and j == 0, stop=closes and j == len(blocks) - 1, is_transpose=True)
+
+        add_turned(old_sb, True, False)
+
+        first, rest = slice(0, FIRST), slice(FIRST, SLOTS)
         scaled = pool.tile([P, SLOTS], F32, name="scaled")
-        for n, c in enumerate(chunks):
-            root = pool.tile([P, CHUNK], F32, name="root%d" % n)
-            nc.scalar.activation(root[:], prods[n][:], ACT.Sqrt, bias=0.1)
-            nc.scalar.activation(scaled[:, c], root[:], ACT.Copy, scale=lam_sb[:])
-            nc.vector.tensor_tensor(f1[n][:].indirect(offs_sb[:, c.start // 16 : c.stop // 16]), scaled[:, c], minus_gap[:, c], ALU.add)
+        root_first = pool.tile([P, FIRST], F32, name="root_first")
+        root_rest = pool.tile([P, SLOTS - FIRST], F32, name="root_rest")
+        w_first = pool.tile([P, FIRST], F32, name="w_first")
+        nc.scalar.activation(root_first[:], prod[:, first], ACT.Sqrt, bias=0.1)
+        nc.vector.scalar_tensor_tensor(w_first[:], root_first[:], lam_sb[:], minus_gap[:, first], ALU.mult, ALU.add)
+        nc.vector.tensor_copy(f1[0][:].indirect(entries(offs_sb, first)), w_first[:])
+        nc.scalar.activation(root_rest[:], prod[:, rest], ACT.Sqrt, bias=0.1)
+        nc.scalar.activation(scaled[:, rest], root_rest[:], ACT.Copy, scale=lam_sb[:])
+        nc.vector.tensor_tensor(f1[1][:].indirect(entries(offs_sb, rest)), scaled[:, rest], minus_gap[:, rest], ALU.add)
+        nc.scalar.activation(scaled[:, first], root_first[:], ACT.Copy, scale=lam_sb[:])
         nc.vector.tensor_tensor(f2[:].indirect(offs2_sb[:]), scaled[:], minus_gap[:], ALU.add)
 
-        for n, part in enumerate(f1):
-            for h in halves:
-                for j in blocks:
-                    t0 = h * BANK + j * P
-                    last = n == len(f1) - 1 and j == len(blocks) - 1
-                    nc.tensor.matmul(turned[h][:, j * P : (j + 1) * P], part[:, t0 : t0 + P], identity[:], start=False, stop=last, is_transpose=True)
-        partial = []
-        for h in halves:
-            turned_sb = pool.tile([P, BANK], F32, name="turned_sb%d" % h)
+        add_turned(f1[0], False, False)
+        add_turned(f1[1], False, True)
+        for h in pieces_out:
+            cols = slice(h * STORE, (h + 1) * STORE)
+            turned_sb = pool.tile([P, STORE], F32, name="turned_sb%d" % h)
             nc.scalar.copy(turned_sb[:], turned[h][:])
-            back = psum.tile([P, BANK], F32, name="back%d" % h)
+            back = psum.tile([P, STORE], F32, name="back%d" % h, tag="bank%d" % (len(pieces_out) + h))
             for j in blocks:
                 nc.tensor.transpose(back[:, j * P : (j + 1) * P], turned_sb[:, j * P : (j + 1) * P], identity[:])
-            partial.append(back)
-        for n, c0 in enumerate(range(0, T, STORE)):
-            cols = slice(c0, c0 + STORE)
-            res = pool.tile([P, STORE], F32, name="res%d" % n)
-            nc.vector.scalar_tensor_tensor(res[:], f2[:, cols], share_sb[:], partial[c0 // BANK][:, c0 % BANK : c0 % BANK + STORE], ALU.mult, ALU.add)
-            queue = nc.sync if n % 2 == 0 else nc.scalar
+            res = pool.tile([P, STORE], F32, name="res%d" % h)
+            nc.vector.scalar_tensor_tensor(res[:], f2[:, cols], share_sb[:], back[:], ALU.mult, ALU.add)
+            queue = nc.sync if h % 2 == 0 else nc.scalar
             queue.dma_start(out=out[:, cols], in_=res[:])

@@ -97,7 +97,7 @@ def tile_attend_agreeingtwo_lean_twiceput_heads_kernel(tc, query, query2, keys_w
         for i in range(2):
             nc.vector.tensor_copy(picked[:, i, :], scores[i][:].indirect(offs_sb[:]))
 
-        prod = pool.tile([P, SLOTS], F32, name="prod")
+        prod = pool.tile([P, SLOTS], F32, name="prod", tag="prod")
         for n, c in enumerate(halves_of_slots):
             logsig = pool.tile([P, 2, CHUNK], F32, name="logsig%d" % n)
             nc.scalar.activation(logsig[:], sig[:, :, c], ACT.Ln, bias=TINY)
@@ -137,7 +137,11 @@ def tile_attend_agreeingtwo_lean_twiceput_heads_kernel(tc, query, query2, keys_w
         nc.scalar.activation(scaled[:, rest], root_rest[:], ACT.Copy, scale=lam_sb[:])
         nc.vector.tensor_tensor(f1[1][:].indirect(entries(offs_sb, rest)), scaled[:, rest], minus_gap[:, rest], ALU.add)
         nc.scalar.activation(scaled[:, first], root_first[:], ACT.Copy, scale=lam_sb[:])
-        nc.vector.tensor_tensor(f2[:].indirect(offs2_sb[:]), scaled[:], minus_gap[:], ALU.add)
+        shared_gap = pool.tile([P, SLOTS], F32, name="shared_gap", tag="prod")
+        nc.scalar.activation(shared_gap[:], minus_gap[:], ACT.Copy, scale=share_sb[:])
+        shared_root = pool.tile([P, SLOTS], F32, name="shared_root")
+        nc.scalar.activation(shared_root[:], scaled[:], ACT.Copy, scale=share_sb[:])
+        nc.vector.tensor_tensor(f2[:].indirect(offs2_sb[:]), shared_root[:], shared_gap[:], ALU.add)
 
         add_turned(f1[0], False, False)
         add_turned(f1[1], False, True)
@@ -149,6 +153,11 @@ def tile_attend_agreeingtwo_lean_twiceput_heads_kernel(tc, query, query2, keys_w
             for j in blocks:
                 nc.tensor.transpose(back[:, j * P : (j + 1) * P], turned_sb[:, j * P : (j + 1) * P], identity[:])
             res = pool.tile([P, STORE], F32, name="res%d" % h)
-            nc.vector.scalar_tensor_tensor(res[:], f2[:, cols], share_sb[:], back[:], ALU.mult, ALU.add)
+            if h == 0:
+                back_sb = pool.tile([P, STORE], F32, name="back_sb")
+                nc.scalar.copy(back_sb[:], back[:])
+                nc.gpsimd.tensor_tensor(res[:], f2[:, cols], back_sb[:], ALU.add)
+            else:
+                nc.vector.tensor_tensor(res[:], f2[:, cols], back[:], ALU.add)
             queue = nc.sync if h % 2 == 0 else nc.scalar
             queue.dma_start(out=out[:, cols], in_=res[:])

from contextlib import ExitStack

import concourse.mybir as mybir
from concourse.masks import make_identity

D, T, SLOTS, Q = 512, 1024, 512, 128
FLOPS = 2 * 2 * D * Q * T

F32 = mybir.dt.float32
BF16 = mybir.dt.bfloat16
I32 = mybir.dt.int32
U16 = mybir.dt.uint16
U8 = mybir.dt.uint8
FP8X4 = mybir.dt.float8_e4m3fn_x4
ACT = mybir.ActivationFunctionType
ALU = mybir.AluOpType

P = 128
PACK = 4
BANK = 512
CHUNK = 256
STORE = 256
FIRST = 128
TINY = 1e-19


def tile_attend_agreeingtwo_lean_twiceput_heads_kernel(tc, query, query2, keys_words, keys_scales, lam, old, share2, offs, offs2, out):
    nc = tc.nc
    with ExitStack() as ctx:
        pool = ctx.enter_context(tc.tile_pool(name="pool", bufs=1))
        psum = ctx.enter_context(tc.psum_pool(name="psum", bufs=1))

        offs_sb = pool.tile([P, SLOTS // 16], U16, name="offs_sb")
        offs2_sb = pool.tile([P, SLOTS // 16], U16, name="offs2_sb")
        key_scale = pool.tile([P, T], U8, name="key_scale", align_bytes=64)
        nc.gpsimd.memset(key_scale[:].bitcast(I32), 0)

        raw = [pool.tile([P, PACK, Q], F32, name="raw%d" % i) for i in range(2)]
        nc.sync.dma_start(out=raw[0][:], in_=query.rearrange("(p j) q -> p j q", j=PACK))
        nc.sync.dma_start(offs_sb[:], offs)
        nc.sync.dma_start(out=raw[1][:], in_=query2.rearrange("(p j) q -> p j q", j=PACK))
        scale_rows = keys_scales[0].bitcast(I32)
        for quad in range(4):
            nc.sync.dma_start(out=key_scale[32 * quad : 32 * quad + 4, :].bitcast(I32), in_=scale_rows[4 * quad : 4 * quad + 4, :])
        words = keys_words[0].rearrange("p n t -> p (n t)").bitcast(I32)
        key_code = [pool.tile([P, BANK], I32, name="key_code%d" % h, tag="key_code%d" % h, align_bytes=64) for h in range(T // BANK)]
        for h, tile in enumerate(key_code):
            nc.sync.dma_start(out=tile[:], in_=words[:, h * BANK : (h + 1) * BANK])
        nc.sync.dma_start(offs2_sb[:], offs2)
        lam_sb = pool.tile([P, 1], F32, name="lam_sb")
        share_sb = pool.tile([P, 1], F32, name="share_sb")
        old_sb = pool.tile([P, T], F32, name="old_sb")
        nc.sync.dma_start(out=lam_sb[:], in_=lam)
        nc.sync.dma_start(out=share_sb[:], in_=share2)
        nc.sync.dma_start(out=old_sb[:], in_=old)

        f1 = [pool.tile([P, T], F32, name="f1_%d" % n) for n in range(SLOTS // CHUNK)]
        for part in f1:
            nc.vector.memset(part[:], 0.0)

        q_code, q_scale = [], []
        for i in range(2):
            grouped = pool.tile([P, Q, PACK], BF16, name="grouped%d" % i, tag="grouped%d" % i, align_bytes=64)
            nc.vector.tensor_copy(out=grouped[:].rearrange("p (c i) j -> p c j i", i=4), in_=raw[i][:].rearrange("p j (c i) -> p c j i", i=4))
            code = pool.tile([P, Q], I32, name="q_code%d" % i, align_bytes=64)
            scale = pool.tile([P, Q], U8, name="q_scale%d" % i, align_bytes=64)
            nc.vector.quantize_mx(out=code[:].bitcast(FP8X4), scales=scale[:], in_=grouped[:].rearrange("p q j -> p (q j)"))
            q_code.append(code)
            q_scale.append(scale)

        f2 = pool.tile([P, T], F32, name="f2", tag="grouped1", align_bytes=64)
        nc.gpsimd.memset(f2[:], 0.0)

        scores = [pool.tile([P, T], F32, name="scores%d" % i) for i in range(2)]
        pieces = ((256, 256, 512), (512, 256, 256))
        banks = 0
        for i in range(2):
            t0 = 0
            for width in pieces[i]:
                cols = slice(t0, t0 + width)
                bank = psum.tile([P, width], F32, name="bank%d" % banks, tag="bank%d" % banks)
                nc.tensor.matmul_mx(out=bank[:], lhsT=q_code[i][:].bitcast(FP8X4), lhsT_scale=q_scale[i][:],
                                    rhs=key_code[t0 // BANK][:, t0 % BANK : t0 % BANK + width].bitcast(FP8X4), rhs_scale=key_scale[:, cols], start=True, stop=True)
                nc.vector.tensor_copy(out=scores[i][:, cols], in_=bank[:])
                t0 += width
                banks += 1

        sig = pool.tile([P, 2, SLOTS], F32, name="sig")
        picked = pool.tile([P, 2, SLOTS], F32, name="picked", tag="key_code1", align_bytes=64)
        halves_of_slots = [slice(c, c + CHUNK) for c in range(0, SLOTS, CHUNK)]

        def entries(tile, slots):
            return tile[:, slots.start // 16 : slots.stop // 16]

        for i in range(2):
            nc.scalar.activation(sig[:, i, :], scores[i][:].indirect(offs_sb[:]), ACT.Sigmoid, scale=-1.0)
        for i in range(2):
            nc.vector.tensor_copy(picked[:, i, :], scores[i][:].indirect(offs_sb[:]))

        prod = pool.tile([P, SLOTS], F32, name="prod", tag="prod")
        for n, c in enumerate(halves_of_slots):
            logsig = pool.tile([P, 2, CHUNK], F32, name="logsig%d" % n)
            nc.scalar.activation(logsig[:], sig[:, :, c], ACT.Ln, bias=TINY)
            soft = pool.tile([P, 2, CHUNK], F32, name="soft%d" % n)
            nc.vector.scalar_tensor_tensor(soft[:], logsig[:], -1.0, picked[:, :, c], ALU.mult, ALU.max)
            nc.vector.tensor_tensor(prod[:, c], soft[:, 0, :], soft[:, 1, :], ALU.mult)

        diff = pool.tile([P, SLOTS], F32, name="diff")
        nc.vector.tensor_tensor(diff[:], picked[:, 0, :], picked[:, 1, :], ALU.subtract)
        minus_gap = pool.tile([P, SLOTS], F32, name="minus_gap")
        nc.vector.scalar_tensor_tensor(minus_gap[:], diff[:], -1.0, diff[:], ALU.mult, ALU.min)

        identity = pool.tile([P, P], F32, name="identity")
        make_identity(nc, identity[:])
        pieces_out = range(T // STORE)
        blocks = range(STORE // P)
        turned = [psum.tile([P, STORE], F32, name="turned%d" % h, tag="bank%d" % h) for h in pieces_out]

        def add_turned(source, opens, closes):
            for h in pieces_out:
                for j in blocks:
                    t0 = h * STORE + j * P
                    nc.tensor.matmul(turned[h][:, j * P : (j + 1) * P], source[:, t0 : t0 + P], identity[:],
                                     start=opens and j == 0, stop=closes and j == len(blocks) - 1, is_transpose=True)

        add_turned(old_sb, True, False)

        first, rest = slice(0, FIRST), slice(FIRST, SLOTS)
        scaled = pool.tile([P, SLOTS], F32, name="scaled")
        root_first = pool.tile([P, FIRST], F32, name="root_first")
        root_rest = pool.tile([P, SLOTS - FIRST], F32, name="root_rest")
        w_first = pool.tile([P, FIRST], F32, name="w_first")
        nc.scalar.activation(root_first[:], prod[:, first], ACT.Sqrt, bias=0.1)
        nc.vector.scalar_tensor_tensor(w_first[:], root_first[:], lam_sb[:], minus_gap[:, first], ALU.mult, ALU.add)
        nc.vector.tensor_copy(f1[0][:].indirect(entries(offs_sb, first)), w_first[:])
        nc.scalar.activation(root_rest[:], prod[:, rest], ACT.Sqrt, bias=0.1)
        nc.scalar.activation(scaled[:, rest], root_rest[:], ACT.Copy, scale=lam_sb[:])
        nc.vector.tensor_tensor(f1[1][:].indirect(entries(offs_sb, rest)), scaled[:, rest], minus_gap[:, rest], ALU.add)
        nc.scalar.activation(scaled[:, first], root_first[:], ACT.Copy, scale=lam_sb[:])
        shared_gap = pool.tile([P, SLOTS], F32, name="shared_gap", tag="prod")
        nc.scalar.activation(shared_gap[:], minus_gap[:], ACT.Copy, scale=share_sb[:])
        shared_root = pool.tile([P, SLOTS], F32, name="shared_root")
        nc.scalar.activation(shared_root[:], scaled[:], ACT.Copy, scale=share_sb[:])
        nc.vector.tensor_tensor(f2[:].indirect(offs2_sb[:]), shared_root[:], shared_gap[:], ALU.add)

        add_turned(f1[0], False, False)
        add_turned(f1[1], False, True)
        for h in pieces_out:
            cols = slice(h * STORE, (h + 1) * STORE)
            turned_sb = pool.tile([P, STORE], F32, name="turned_sb%d" % h)
            nc.scalar.copy(turned_sb[:], turned[h][:])
            back = psum.tile([P, STORE], F32, name="back%d" % h, tag="bank%d" % (len(pieces_out) + h))
            for j in blocks:
                nc.tensor.transpose(back[:, j * P : (j + 1) * P], turned_sb[:, j * P : (j + 1) * P], identity[:])
            res = pool.tile([P, STORE], F32, name="res%d" % h)
            if h == 0:
                back_sb = pool.tile([P, STORE], F32, name="back_sb")
                nc.scalar.copy(back_sb[:], back[:])
                nc.gpsimd.tensor_tensor(res[:], f2[:, cols], back_sb[:], ALU.add)
            else:
                nc.vector.tensor_tensor(res[:], f2[:, cols], back[:], ALU.add)
            queue = nc.sync if h % 2 == 0 else nc.scalar
            queue.dma_start(out=out[:, cols], in_=res[:])
